import numpy as np
import ml_dtypes


def mxq(x, axis, fmt="e4m3"):
    dtype, down = {"e4m3": (ml_dtypes.float8_e4m3fn, 7), "e5m2": (ml_dtypes.float8_e5m2, 14)}[fmt]
    v = np.moveaxis(np.asarray(x, np.float32).astype(ml_dtypes.bfloat16).astype(np.float64), axis, -1)
    blocks = v.reshape(v.shape[:-1] + (-1, 32))
    amax = np.abs(blocks).max(-1, keepdims=True)
    byte = np.maximum(np.where(amax > 0, np.frexp(amax)[1] - 1 + 127, 0) - down, 1)
    scale = np.exp2(byte - 127.0)
    codes = (blocks / scale).astype(np.float32).astype(dtype).astype(np.float64)
    return np.moveaxis((codes * scale).reshape(v.shape), -1, axis)


WIDE = False


def mx_kscale(k):
    if not WIDE:
        return np.ones(k)
    levels = np.array([10, -10, 5, -5, 0])
    if k % 512:
        return np.exp2(np.random.permutation(np.resize(levels, k // 32))).repeat(32)
    a = np.empty((k // 512, 16))
    for p in range(k // 512):
        a[p, :8] = np.random.permutation(np.resize(levels, 8))
        for g in range(8):
            far = levels[np.abs(levels - a[p, g]) >= 10]
            a[p, g + 8] = far[np.random.randint(len(far))]
    return np.exp2(a.ravel()).repeat(32)


def f64(x):
    return np.asarray(x).astype(np.float64)


def striped(idx):
    return np.tile(idx.reshape(-1, 16).T, (8, 1)).astype(np.uint16)


def unstriped(offs):
    return offs[:16].T.reshape(-1).astype(np.int64)


def gelu(v):
    return 0.5 * v * (1.0 + np.tanh(np.sqrt(2.0 / np.pi) * (v + 0.044715 * v**3)))


K, T, D, S, V, N = 1024, 2048, 4, 2048, 512, 256
P = 2 ** 7


def setup_inputs():
    n = np.random.standard_normal
    s = mx_kscale(K)[:, None]
    return {
        "xT": (n((K, T)) * s / np.sqrt(D)).astype(ml_dtypes.bfloat16).astype(np.float32),
        "w": (n((K, N)) / np.sqrt(K) / s).astype(np.float32),
        "b": (0.3 * n((N, 1))).astype(np.float32),
        "gate": np.tile(np.random.uniform(0.5, 1.5, (D, 1, V)), (1, P, 1)).astype(ml_dtypes.bfloat16).astype(np.float32),
        "offs": striped(np.concatenate([np.random.permutation(T)[:V] for _ in range(D)])),
    }


def reference(xT, w, b, gate, offs):
    idx = unstriped(offs)
    x = sum(f64(gate)[d, :1] * f64(xT)[:, idx[d * V:(d + 1) * V]] for d in range(D))
    return gelu((mxq(f64(w), 0, "e4m3").T @ mxq(x, 0, "e4m3")) + f64(b))

@@ -1,0 +1,213 @@
+from contextlib import ExitStack
+
+import concourse.mybir as mybir
+from concourse.masks import make_identity
+
+K, T, D, V, N = 1024, 2048, 4, 512, 256
+FLOPS = 2 * K * N * V
+
+F32 = mybir.dt.float32
+BF16 = mybir.dt.bfloat16
+U32 = mybir.dt.uint32
+U16 = mybir.dt.uint16
+U8 = mybir.dt.uint8
+FP8X4 = mybir.dt.float8_e4m3fn_x4
+ACT = mybir.ActivationFunctionType
+MULT = mybir.AluOpType.mult
+
+P = 128
+PASSES = 2
+BLOCKS = V // P
+HALF = V // 2
+BIAS_ROW = D
+CHUNKS = [[512, 512, 512, 512], [1024, 1024], [1024, 1024], [1024, 1024]]
+
+
+def tile_picked_bag_lin_gelu_sub_l_kernel(tc, xT, w, b, gate, offs, out):
+    nc = tc.nc
+    with ExitStack() as ctx:
+        keep = ctx.enter_context(tc.tile_pool(name="keep", bufs=1))
+        ring = ctx.enter_context(tc.tile_pool(name="ring", bufs=1))
+        psum = ctx.enter_context(tc.psum_pool(name="psum", bufs=4))
+
+        offsets = keep.tile([P, D * V // 16], U16, name="offsets")
+        ident = keep.tile([P, P], F32, name="ident")
+        rows = keep.tile([P, V], F32, name="rows")
+        cols = keep.tile([P, BLOCKS, 8], F32, name="cols")
+        scratch = keep.tile([P, 8], F32, name="scratch")
+        windows = [keep.tile([P, T], U32, name="window%d" % q) for q in range(4)]
+        w_raw = keep.tile([P, PASSES, 4, N], F32, name="w_raw")
+        w_bf = keep.tile([P, PASSES, N, 4], BF16, name="w_bf", align_bytes=64)
+        w_codes = keep.tile([P, PASSES * N], U32, name="w_codes", align_bytes=64)
+        w_scales = keep.tile([P, PASSES * N], U8, name="w_scales", align_bytes=64)
+        x_bf = [keep.tile([P, V, 4], BF16, name="x_bf%d" % g, align_bytes=64) for g in range(PASSES)]
+        x_codes = [keep.tile([P, V], U32, name="x_codes%d" % g, align_bytes=64) for g in range(PASSES)]
+        x_scales = [keep.tile([P, V], U8, name="x_scales%d" % g, align_bytes=64) for g in range(PASSES)]
+
+        nc.gpsimd.memset(rows[:], 0.0)
+        raw = {}
+        for q in range(4):
+            g, u = divmod(q, 2)
+            src = xT[g * 512 : (g + 1) * 512, :].rearrange("(p j) t -> p j t", j=4)
+            start = 0
+            for c, width in enumerate(CHUNKS[q]):
+                chunk = keep.tile([P, 2, width], F32, name="raw%d_%d" % (q, c))
+                nc.sync.dma_start(out=chunk[:], in_=src[:, 2 * u : 2 * u + 2, start : start + width])
+                raw[q, c] = (chunk, start, width)
+                start += width
+                if (q, c) == (0, 0):
+                    nc.sync.dma_start(out=rows[0:D, :], in_=gate[:, 0, :])
+                    nc.sync.dma_start(out=rows[BIAS_ROW : BIAS_ROW + 1, 0:N], in_=b.rearrange("n o -> o n"))
+                    nc.sync.dma_start(offsets[:], offs)
+        for g in range(PASSES):
+            nc.sync.dma_start(
+                out=w_raw[:, g, :, :], in_=w[g * 512 : (g + 1) * 512, :].rearrange("(p j) n -> p j n", j=4)
+            )
+
+        nc.vector.memset(scratch[:], 0.0)
+        nc.scalar.activation(scratch[:, 1:2], scratch[:, 0:1], ACT.Gelu_apprx_tanh)
+        make_identity(nc, ident[:])
+        turned = psum.tile([P, BLOCKS, P], F32, tag="flip", name="turned")
+        for j in range(BLOCKS):
+            nc.tensor.transpose(turned[:, j, :], rows[:, j * P : (j + 1) * P], ident[:])
+        nc.scalar.copy(cols[:], turned[:, :, 0:8])
+
+        def cast(q, c):
+            chunk, start, width = raw[q, c]
+            pairs = windows[q][:, start : start + width].bitcast(BF16).rearrange("p (t i) -> p t i", i=2)
+            nc.vector.tensor_copy(out=pairs, in_=chunk[:].rearrange("p i t -> p t i"))
+
+        products = {}
+
+        def weigh(q, d, j, bank, slot, engine):
+            product = ring.tile([P, 2, P], F32, tag="product", bufs=40, name="product")
+            values = bank[:, slot, :].bitcast(BF16).rearrange("e (p i) -> e i p", i=2)
+            if engine == "scalar":
+                nc.scalar.activation(product[:], values, ACT.Copy, scale=cols[:, j, d : d + 1])
+            else:
+                nc.vector.tensor_scalar(product[:], values, cols[:, j, d : d + 1], None, MULT)
+            products[q, d, j] = product
+
+        def look_up(q, d, blocks, split):
+            count = len(blocks) * P
+            first = (d * V + blocks[0] * P) // 16
+            picked = ring.tile([P, count], U32, tag="picked", bufs=4, name="picked")
+            nc.vector.tensor_copy(picked[:], windows[q][:].indirect(offsets[:, first : first + count // 16]))
+            words = picked[:].bitcast(F32)
+            if split:
+                for s, j in enumerate(blocks):
+                    bank = psum.tile([P, 1, P], F32, tag="flip", name="flip")
+                    nc.tensor.transpose(bank[:, 0, :], words[:, s * P : (s + 1) * P], ident[:])
+                    weigh(q, d, j, bank, 0, "scalar" if s == 0 else "vector")
+            else:
+                bank = psum.tile([P, len(blocks), P], F32, tag="flip", name="flip")
+                for s, j in enumerate(blocks):
+                    nc.tensor.transpose(bank[:, s, :], words[:, s * P : (s + 1) * P], ident[:])
+                for s, j in enumerate(blocks):
+                    weigh(q, d, j, bank, s, "scalar")
+
+        sums = {}
+
+        def add_up(q, j):
+            g, u = divmod(q, 2)
+            if u == 0:
+                sums[g, j] = psum.tile([P, 4, P], F32, tag="acc", name="acc")
+            for i in range(2):
+                for d in range(D):
+                    nc.tensor.matmul(
+                        sums[g, j][:, 2 * u + i, :],
+                        products[q, d, j][:, i, :],
+                        ident[:],
+                        start=(d == 0),
+                        stop=(d == D - 1),
+                        is_transpose=True,
+                    )
+
+        def round_sums(g, j, engine):
+            dst = x_bf[g][:, j * P : (j + 1) * P, :]
+            src = sums[g, j][:].rearrange("p t c -> p c t")
+            if engine == "scalar":
+                nc.scalar.copy(dst, src)
+            else:
+                nc.vector.tensor_copy(dst, src)
+
+        def quantise_x(g, start, width):
+            nc.vector.quantize_mx(
+                out=x_codes[g][:, start : start + width].bitcast(FP8X4),
+                scales=x_scales[g][:, start : start + width],
+                in_=x_bf[g][:, start : start + width, :].rearrange("p v t -> p (v t)"),
+            )
+
+        def product_pass(acc, m, h, g):
+            wc = slice(g * N + m * P, g * N + (m + 1) * P)
+            xc = slice(h * HALF, (h + 1) * HALF)
+            nc.tensor.matmul_mx(
+                out=acc[:],
+                lhsT=w_codes[:, wc].bitcast(FP8X4),
+                lhsT_scale=w_scales[:, wc],
+                rhs=x_codes[g][:, xc].bitcast(FP8X4),
+                rhs_scale=x_scales[g][:, xc],
+                start=(g == 0),
+                stop=(g == PASSES - 1),
+            )
+
+        def finish(acc, m, h):
+            result = keep.tile([P, HALF], F32, name="result%d_%d" % (m, h))
+            nc.scalar.activation(
+                result[:], acc[:], ACT.Gelu_apprx_tanh, bias=cols[:, m, BIAS_ROW : BIAS_ROW + 1]
+            )
+            nc.sync.dma_start(out=out[m * P : (m + 1) * P, h * HALF : (h + 1) * HALF], in_=result[:])
+
+        for c in range(len(CHUNKS[0])):
+            cast(0, c)
+        for q in range(3):
+            for d in range(D):
+                look_up(q, d, [0, 1, 2, 3], False)
+                if d % 2 == 1:
+                    cast(q + 1, d // 2)
+            if q > 0:
+                for j in range(BLOCKS):
+                    add_up(q - 1, j)
+                    if q == 2:
+                        round_sums(0, j, "scalar")
+
+        nc.vector.tensor_copy(out=w_bf[:], in_=w_raw[:].rearrange("p g j n -> p g n j"))
+        for d in range(D):
+            look_up(3, d, [0, 1], False)
+            if d == 0:
+                quantise_x(0, 0, V)
+            if d == 1:
+                nc.vector.quantize_mx(
+                    out=w_codes[:].bitcast(FP8X4),
+                    scales=w_scales[:],
+                    in_=w_bf[:].rearrange("p g n j -> p (g n j)"),
+                )
+        for j in range(BLOCKS):
+            add_up(2, j)
+        for d in range(D):
+            look_up(3, d, [2, 3], d == D - 1)
+
+        late = [psum.tile([P, HALF], F32, tag="flip", name="late") for m in range(2)]
+        for m in range(2):
+            product_pass(late[m], m, 1, 0)
+
+        for j in (0, 1):
+            add_up(3, j)
+        for j in (2, 3):
+            add_up(3, j)
+        round_sums(1, 0, "vector")
+        round_sums(1, 1, "scalar")
+        quantise_x(1, 0, HALF)
+        round_sums(1, 2, "scalar")
+        round_sums(1, 3, "vector")
+        quantise_x(1, HALF, HALF)
+        early = [psum.tile([P, HALF], F32, tag="acc", name="early") for m in range(2)]
+        for m in range(2):
+            for g in range(PASSES):
+                product_pass(early[m], m, 0, g)
+        for m in range(2):
+            product_pass(late[m], m, 1, 1)
+        for m in range(2):
+            finish(early[m], m, 0)
+        for m in range(2):
+            finish(late[m], m, 1)

@@ -14,13 +14,15 @@ U8 = mybir.dt.uint8
 FP8X4 = mybir.dt.float8_e4m3fn_x4
 ACT = mybir.ActivationFunctionType
 MULT = mybir.AluOpType.mult
+ADD = mybir.AluOpType.add
 
 P = 128
 PASSES = 2
 BLOCKS = V // P
 HALF = V // 2
 BIAS_ROW = D
-CHUNKS = [[512, 512, 512, 512], [1024, 1024], [1024, 1024], [1024, 1024]]
+CHUNKS = [[512, 512, 512, 256, 256], [1024, 512, 512], [1024, 512, 512], [1024, 512, 512]]
+CAST = 512
 
 
 def tile_picked_bag_lin_gelu_sub_l_kernel(tc, xT, w, b, gate, offs, out):
@@ -77,6 +79,15 @@ def tile_picked_bag_lin_gelu_sub_l_kernel(tc, xT, w, b, gate, offs, out):
             pairs = windows[q][:, start : start + width].bitcast(BF16).rearrange("p (t i) -> p t i", i=2)
             nc.vector.tensor_copy(out=pairs, in_=chunk[:].rearrange("p i t -> p t i"))
 
+        def cast_pool(q):
+            for c in range(len(CHUNKS[q])):
+                chunk, start, width = raw[q, c]
+                for a in range(0, width, CAST):
+                    pairs = windows[q][:, start + a : start + a + CAST].bitcast(BF16).rearrange("p (t i) -> p t i", i=2)
+                    nc.gpsimd.tensor_scalar(
+                        pairs, chunk[:, :, a : a + CAST].rearrange("p i t -> p t i"), 1.0, 0.0, MULT, ADD
+                    )
+
         products = {}
 
         def weigh(q, d, j, bank, slot, engine):
@@ -108,18 +119,18 @@ def tile_picked_bag_lin_gelu_sub_l_kernel(tc, xT, w, b, gate, offs, out):
 
         sums = {}
 
-        def add_up(q, j):
+        def add_up(q, d, blocks):
             g, u = divmod(q, 2)
-            if u == 0:
-                sums[g, j] = psum.tile([P, 4, P], F32, tag="acc", name="acc")
-            for i in range(2):
-                for d in range(D):
+            for j in blocks:
+                if u == 0 and d == 0:
+                    sums[g, j] = psum.tile([P, 4, P], F32, tag="acc", name="acc")
+                for i in range(2):
                     nc.tensor.matmul(
                         sums[g, j][:, 2 * u + i, :],
                         products[q, d, j][:, i, :],
                         ident[:],
-                        start=(d == 0),
-                        stop=(d == D - 1),
+                        start=(u == 0 and d == 0 and i == 0),
+                        stop=(u == 1 and d == D - 1 and i == 1),
                         is_transpose=True,
                     )
 
@@ -160,43 +171,34 @@ def tile_picked_bag_lin_gelu_sub_l_kernel(tc, xT, w, b, gate, offs, out):
 
         for c in range(len(CHUNKS[0])):
             cast(0, c)
-        for q in range(3):
-            for d in range(D):
-                look_up(q, d, [0, 1, 2, 3], False)
-                if d % 2 == 1:
-                    cast(q + 1, d // 2)
-            if q > 0:
-                for j in range(BLOCKS):
-                    add_up(q - 1, j)
-                    if q == 2:
-                        round_sums(0, j, "scalar")
+        for q in range(1, 4):
+            cast_pool(q)
+        nc.gpsimd.tensor_scalar(w_bf[:], w_raw[:].rearrange("p g j n -> p g n j"), 1.0, 0.0, MULT, ADD)
 
-        nc.vector.tensor_copy(out=w_bf[:], in_=w_raw[:].rearrange("p g j n -> p g n j"))
-        for d in range(D):
-            look_up(3, d, [0, 1], False)
-            if d == 0:
+        pieces = [(q, d, [0, 1, 2, 3]) for q in range(3) for d in range(D)]
+        pieces += [(3, d, blocks) for blocks in ([0, 1], [2, 3]) for d in range(D)]
+        for n, (q, d, blocks) in enumerate(pieces):
+            look_up(q, d, blocks, n == len(pieces) - 1)
+            if n > 0:
+                add_up(*pieces[n - 1])
+            if n == 8:
+                for j in range(BLOCKS):
+                    round_sums(0, j, "vector")
+            if n == 10:
                 quantise_x(0, 0, V)
-            if d == 1:
+            if n == 15:
                 nc.vector.quantize_mx(
                     out=w_codes[:].bitcast(FP8X4),
                     scales=w_scales[:],
                     in_=w_bf[:].rearrange("p g n j -> p (g n j)"),
                 )
-        for j in range(BLOCKS):
-            add_up(2, j)
-        for d in range(D):
-            look_up(3, d, [2, 3], d == D - 1)
-
+            if n == 17:
+                round_sums(1, 0, "scalar")
+                round_sums(1, 1, "vector")
+        add_up(*pieces[-1])
         late = [psum.tile([P, HALF], F32, tag="flip", name="late") for m in range(2)]
         for m in range(2):
             product_pass(late[m], m, 1, 0)
-
-        for j in (0, 1):
-            add_up(3, j)
-        for j in (2, 3):
-            add_up(3, j)
-        round_sums(1, 0, "vector")
-        round_sums(1, 1, "scalar")
         quantise_x(1, 0, HALF)
         round_sums(1, 2, "scalar")
         round_sums(1, 3, "vector")

@@ -21,8 +21,17 @@ PASSES = 2
 BLOCKS = V // P
 HALF = V // 2
 BIAS_ROW = D
-CHUNKS = [[512, 512, 512, 256, 256], [1024, 512, 512], [1024, 512, 512], [1024, 512, 512]]
-CAST = 512
+CHUNKS = [[512, 512, 512, 256, 256], [768, 768, 512], [256, 768, 1024], [256, 1024, 768]]
+SHARES = [None, [384, 128, 256], [256, 256, 512], [256, 128, 0]]
+DIRECT = 3
+FUSED = []
+LAST = [2, 2]
+W_AFTER = 3
+PICKED = 3
+DIRECT_TAG = ['raw1_2', 'raw3_1']
+HOLD = True
+MARK = (3, 0, 2)
+W_TAG = 'mark'
 
 
 def tile_picked_bag_lin_gelu_sub_l_kernel(tc, xT, w, b, gate, offs, out):
@@ -40,11 +49,12 @@ def tile_picked_bag_lin_gelu_sub_l_kernel(tc, xT, w, b, gate, offs, out):
         windows = [keep.tile([P, T], U32, name="window%d" % q) for q in range(4)]
         w_raw = keep.tile([P, PASSES, 4, N], F32, name="w_raw")
         w_bf = keep.tile([P, PASSES, N, 4], BF16, name="w_bf", align_bytes=64)
-        w_codes = keep.tile([P, PASSES * N], U32, name="w_codes", align_bytes=64)
         w_scales = keep.tile([P, PASSES * N], U8, name="w_scales", align_bytes=64)
         x_bf = [keep.tile([P, V, 4], BF16, name="x_bf%d" % g, align_bytes=64) for g in range(PASSES)]
         x_codes = [keep.tile([P, V], U32, name="x_codes%d" % g, align_bytes=64) for g in range(PASSES)]
         x_scales = [keep.tile([P, V], U8, name="x_scales%d" % g, align_bytes=64) for g in range(PASSES)]
+
+        gate_pairs = keep.tile([P, V, 2], F32, name="gate_pairs")
 
         nc.gpsimd.memset(rows[:], 0.0)
         raw = {}
@@ -61,10 +71,11 @@ def tile_picked_bag_lin_gelu_sub_l_kernel(tc, xT, w, b, gate, offs, out):
                     nc.sync.dma_start(out=rows[0:D, :], in_=gate[:, 0, :])
                     nc.sync.dma_start(out=rows[BIAS_ROW : BIAS_ROW + 1, 0:N], in_=b.rearrange("n o -> o n"))
                     nc.sync.dma_start(offsets[:], offs)
-        for g in range(PASSES):
-            nc.sync.dma_start(
-                out=w_raw[:, g, :, :], in_=w[g * 512 : (g + 1) * 512, :].rearrange("(p j) n -> p j n", j=4)
-            )
+            if q == W_AFTER:
+                for g in range(PASSES):
+                    nc.sync.dma_start(
+                        out=w_raw[:, g, :, :], in_=w[g * 512 : (g + 1) * 512, :].rearrange("(p j) n -> p j n", j=4)
+                    )
 
         nc.vector.memset(scratch[:], 0.0)
         nc.scalar.activation(scratch[:, 1:2], scratch[:, 0:1], ACT.Gelu_apprx_tanh)
@@ -73,20 +84,51 @@ def tile_picked_bag_lin_gelu_sub_l_kernel(tc, xT, w, b, gate, offs, out):
         for j in range(BLOCKS):
             nc.tensor.transpose(turned[:, j, :], rows[:, j * P : (j + 1) * P], ident[:])
         nc.scalar.copy(cols[:], turned[:, :, 0:8])
+        spread = psum.tile([P, V], F32, tag="flip", name="spread")
+        for j in range(BLOCKS):
+            nc.tensor.transpose(
+                spread[:, j * P : (j + 1) * P], cols[:, j, DIRECT : DIRECT + 1].to_broadcast([P, P]), ident[:]
+            )
+        nc.scalar.copy(gate_pairs[:], spread[:].unsqueeze(2).to_broadcast([P, V, 2]))
 
         def cast(q, c):
             chunk, start, width = raw[q, c]
             pairs = windows[q][:, start : start + width].bitcast(BF16).rearrange("p (t i) -> p t i", i=2)
             nc.vector.tensor_copy(out=pairs, in_=chunk[:].rearrange("p i t -> p t i"))
 
-        def cast_pool(q):
-            for c in range(len(CHUNKS[q])):
-                chunk, start, width = raw[q, c]
-                for a in range(0, width, CAST):
-                    pairs = windows[q][:, start + a : start + a + CAST].bitcast(BF16).rearrange("p (t i) -> p t i", i=2)
-                    nc.gpsimd.tensor_scalar(
-                        pairs, chunk[:, :, a : a + CAST].rearrange("p i t -> p t i"), 1.0, 0.0, MULT, ADD
-                    )
+        def cast_shared(q, c, engine):
+            chunk, start, width = raw[q, c]
+            share = SHARES[q][c]
+            a, z = (0, share) if engine == "scalar" else (share, width)
+            if z > a:
+                pairs = windows[q][:, start + a : start + z].bitcast(BF16).rearrange("p (t i) -> p t i", i=2)
+                values = chunk[:, :, a:z].rearrange("p i t -> p t i")
+                if engine == "scalar":
+                    nc.scalar.copy(pairs, values)
+                else:
+                    nc.gpsimd.tensor_scalar(pairs, values, 1.0, 0.0, MULT, ADD)
+
+        held = {}
+        direct = {}
+
+        def look_up_direct(q):
+            picked = keep.tile([P, V], U32, name="held%d" % q)
+            first = DIRECT * V // 16
+            nc.vector.tensor_copy(picked[:], windows[q][:].indirect(offsets[:, first : first + V // 16]))
+            held[q] = picked
+
+        def weigh_direct(q, start, width):
+            g, u = divmod(q, 2)
+            if g not in direct:
+                direct[g] = keep.tile([P, 2, V, 2], F32, name="direct%d" % g, tag=DIRECT_TAG[g])
+            if q == 1 and HOLD:
+                nc.gpsimd.tensor_copy(direct[g][:, u, 0, :], windows[2][:, T - 1 : T].bitcast(BF16))
+            nc.gpsimd.tensor_tensor(
+                direct[g][:, u, start : start + width, :].rearrange("p v i -> p (v i)"),
+                held[q][:, start : start + width].bitcast(BF16),
+                gate_pairs[:, start : start + width, :].rearrange("p v i -> p (v i)"),
+                MULT,
+            )
 
         products = {}
 
@@ -95,14 +137,27 @@ def tile_picked_bag_lin_gelu_sub_l_kernel(tc, xT, w, b, gate, offs, out):
             values = bank[:, slot, :].bitcast(BF16).rearrange("e (p i) -> e i p", i=2)
             if engine == "scalar":
                 nc.scalar.activation(product[:], values, ACT.Copy, scale=cols[:, j, d : d + 1])
+            elif engine == "fused":
+                nc.vector.scalar_tensor_tensor(
+                    product[:], values, cols[:, j, d : d + 1], products.pop((q, d - 1, j))[:], MULT, ADD
+                )
             else:
                 nc.vector.tensor_scalar(product[:], values, cols[:, j, d : d + 1], None, MULT)
             products[q, d, j] = product
 
+        banks = {}
+
+        def weigh_bank(q, d, blocks, engine):
+            for s, j in enumerate(blocks):
+                weigh(q, d, j, banks[q, d], s, engine)
+
         def look_up(q, d, blocks, split):
             count = len(blocks) * P
             first = (d * V + blocks[0] * P) // 16
-            picked = ring.tile([P, count], U32, tag="picked", bufs=4, name="picked")
+            if (q, d, blocks[0]) == MARK:
+                picked = keep.tile([P, count], U32, tag="mark", name="picked", align_bytes=64)
+            else:
+                picked = ring.tile([P, count], U32, tag="picked", bufs=PICKED, name="picked")
             nc.vector.tensor_copy(picked[:], windows[q][:].indirect(offsets[:, first : first + count // 16]))
             words = picked[:].bitcast(F32)
             if split:
@@ -114,33 +169,61 @@ def tile_picked_bag_lin_gelu_sub_l_kernel(tc, xT, w, b, gate, offs, out):
                 bank = psum.tile([P, len(blocks), P], F32, tag="flip", name="flip")
                 for s, j in enumerate(blocks):
                     nc.tensor.transpose(bank[:, s, :], words[:, s * P : (s + 1) * P], ident[:])
-                for s, j in enumerate(blocks):
-                    weigh(q, d, j, bank, s, "scalar")
+                banks[q, d] = bank
+                if (q, d) not in FUSED:
+                    weigh_bank(q, d, blocks, "scalar")
 
         sums = {}
 
         def add_up(q, d, blocks):
             g, u = divmod(q, 2)
             for j in blocks:
-                if u == 0 and d == 0:
+                fresh = (g, j) not in sums
+                if fresh:
                     sums[g, j] = psum.tile([P, 4, P], F32, tag="acc", name="acc")
                 for i in range(2):
                     nc.tensor.matmul(
                         sums[g, j][:, 2 * u + i, :],
                         products[q, d, j][:, i, :],
                         ident[:],
-                        start=(u == 0 and d == 0 and i == 0),
-                        stop=(u == 1 and d == D - 1 and i == 1),
+                        start=(fresh and i == 0),
+                        stop=(u == 1 and d == LAST[g] and i == 1),
                         is_transpose=True,
                     )
 
-        def round_sums(g, j, engine):
+        def round_plain(g, j, engine):
             dst = x_bf[g][:, j * P : (j + 1) * P, :]
             src = sums[g, j][:].rearrange("p t c -> p c t")
             if engine == "scalar":
                 nc.scalar.copy(dst, src)
             else:
                 nc.vector.tensor_copy(dst, src)
+
+        late_tiles = {}
+
+        def quantise_w():
+            w_codes = keep.tile([P, PASSES * N], U32, name="w_codes", align_bytes=64, tag=W_TAG)
+            late_tiles["w"] = w_codes
+            nc.vector.quantize_mx(
+                out=w_codes[:].bitcast(FP8X4),
+                scales=w_scales[:],
+                in_=w_bf[:].rearrange("p g n j -> p (g n j)"),
+            )
+
+        def round_sums(g, j):
+            nc.vector.tensor_tensor(
+                x_bf[g][:, j * P : (j + 1) * P, :].rearrange("p c (u i) -> p c u i", i=2),
+                sums[g, j][:].rearrange("p (u i) c -> p c u i", i=2),
+                direct[g][:, :, j * P : (j + 1) * P, :].rearrange("p u c i -> p c u i"),
+                ADD,
+            )
+
+        def cast_w(g, engine):
+            values = w_raw[:, g, :, :].rearrange("p j n -> p n j")
+            if engine == "scalar":
+                nc.scalar.copy(w_bf[:, g, :, :], values)
+            else:
+                nc.gpsimd.tensor_scalar(w_bf[:, g, :, :], values, 1.0, 0.0, MULT, ADD)
 
         def quantise_x(g, start, width):
             nc.vector.quantize_mx(
@@ -154,7 +237,7 @@ def tile_picked_bag_lin_gelu_sub_l_kernel(tc, xT, w, b, gate, offs, out):
             xc = slice(h * HALF, (h + 1) * HALF)
             nc.tensor.matmul_mx(
                 out=acc[:],
-                lhsT=w_codes[:, wc].bitcast(FP8X4),
+                lhsT=late_tiles["w"][:, wc].bitcast(FP8X4),
                 lhsT_scale=w_scales[:, wc],
                 rhs=x_codes[g][:, xc].bitcast(FP8X4),
                 rhs_scale=x_scales[g][:, xc],
@@ -169,47 +252,93 @@ def tile_picked_bag_lin_gelu_sub_l_kernel(tc, xT, w, b, gate, offs, out):
             )
             nc.sync.dma_start(out=out[m * P : (m + 1) * P, h * HALF : (h + 1) * HALF], in_=result[:])
 
-        for c in range(len(CHUNKS[0])):
-            cast(0, c)
-        for q in range(1, 4):
-            cast_pool(q)
-        nc.gpsimd.tensor_scalar(w_bf[:], w_raw[:].rearrange("p g j n -> p g n j"), 1.0, 0.0, MULT, ADD)
-
-        pieces = [(q, d, [0, 1, 2, 3]) for q in range(3) for d in range(D)]
-        pieces += [(3, d, blocks) for blocks in ([0, 1], [2, 3]) for d in range(D)]
-        for n, (q, d, blocks) in enumerate(pieces):
-            look_up(q, d, blocks, n == len(pieces) - 1)
-            if n > 0:
-                add_up(*pieces[n - 1])
-            if n == 8:
-                for j in range(BLOCKS):
-                    round_sums(0, j, "vector")
-            if n == 10:
-                quantise_x(0, 0, V)
-            if n == 15:
-                nc.vector.quantize_mx(
-                    out=w_codes[:].bitcast(FP8X4),
-                    scales=w_scales[:],
-                    in_=w_bf[:].rearrange("p g n j -> p (g n j)"),
-                )
-            if n == 17:
-                round_sums(1, 0, "scalar")
-                round_sums(1, 1, "vector")
-        add_up(*pieces[-1])
+        cast(0, 0)
+        cast(0, 1)
+        cast(0, 2)
+        cast(0, 3)
+        cast(0, 4)
+        cast_shared(1, 0, "pool")
+        cast_shared(1, 0, "scalar")
+        cast_shared(1, 1, "scalar")
+        cast_shared(2, 0, "pool")
+        cast_shared(2, 0, "scalar")
+        cast_shared(2, 1, "scalar")
+        look_up(0, 0, [0, 1, 2, 3], False)
+        cast_shared(1, 1, "pool")
+        cast_shared(1, 2, "scalar")
+        cast_shared(3, 0, "pool")
+        look_up(0, 1, [0, 1, 2, 3], False)
+        add_up(0, 0, [0, 1, 2, 3])
+        look_up(0, 2, [0, 1, 2, 3], False)
+        add_up(0, 1, [0, 1, 2, 3])
+        cast_shared(1, 2, "pool")
+        cast_shared(3, 1, "pool")
+        look_up_direct(0)
+        weigh_direct(0, 0, V)
+        add_up(0, 2, [0, 1, 2, 3])
+        cast_shared(2, 1, "pool")
+        cast_shared(2, 2, "scalar")
+        look_up(1, 0, [0, 1, 2, 3], False)
+        cast_shared(2, 2, "pool")
+        look_up(1, 1, [0, 1, 2, 3], False)
+        add_up(1, 0, [0, 1, 2, 3])
+        cast_shared(3, 0, "scalar")
+        look_up(1, 2, [0, 1, 2, 3], False)
+        add_up(1, 1, [0, 1, 2, 3])
+        cast_shared(3, 1, "scalar")
+        look_up_direct(1)
+        weigh_direct(1, 0, V)
+        add_up(1, 2, [0, 1, 2, 3])
+        cast_w(1, "pool")
+        look_up(2, 0, [0, 1, 2, 3], False)
+        look_up(2, 1, [0, 1, 2, 3], False)
+        cast_shared(3, 2, "scalar")
+        look_up(2, 2, [0, 1, 2, 3], False)
+        round_sums(0, 0)
+        round_sums(0, 1)
+        cast_shared(3, 2, "pool")
+        look_up_direct(2)
+        weigh_direct(2, 0, V)
+        round_sums(0, 2)
+        round_sums(0, 3)
+        cast_w(0, "pool")
+        look_up_direct(3)
+        weigh_direct(3, 0, HALF)
+        weigh_direct(3, HALF, HALF)
+        add_up(2, 0, [0, 1, 2, 3])
+        add_up(2, 1, [0, 1, 2, 3])
+        add_up(2, 2, [0, 1, 2, 3])
+        look_up(3, 0, [0, 1], False)
+        look_up(3, 1, [0, 1], False)
+        add_up(3, 0, [0, 1])
+        quantise_x(0, 0, V)
+        look_up(3, 2, [0, 1], False)
+        add_up(3, 1, [0, 1])
+        look_up(3, 0, [2, 3], False)
+        add_up(3, 2, [0, 1])
+        round_sums(1, 0)
+        look_up(3, 1, [2, 3], False)
+        add_up(3, 0, [2, 3])
+        quantise_w()
+        look_up(3, 2, [2, 3], True)
+        add_up(3, 1, [2, 3])
+        round_sums(1, 1)
+        add_up(3, 2, [2, 3])
         late = [psum.tile([P, HALF], F32, tag="flip", name="late") for m in range(2)]
-        for m in range(2):
-            product_pass(late[m], m, 1, 0)
-        quantise_x(1, 0, HALF)
-        round_sums(1, 2, "scalar")
-        round_sums(1, 3, "vector")
-        quantise_x(1, HALF, HALF)
         early = [psum.tile([P, HALF], F32, tag="acc", name="early") for m in range(2)]
-        for m in range(2):
-            for g in range(PASSES):
-                product_pass(early[m], m, 0, g)
-        for m in range(2):
-            product_pass(late[m], m, 1, 1)
-        for m in range(2):
-            finish(early[m], m, 0)
-        for m in range(2):
-            finish(late[m], m, 1)
+        quantise_x(1, 0, HALF)
+        round_sums(1, 3)
+        round_sums(1, 2)
+        product_pass(late[0], 0, 1, 0)
+        product_pass(late[1], 1, 1, 0)
+        product_pass(early[0], 0, 0, 0)
+        product_pass(early[0], 0, 0, 1)
+        product_pass(early[1], 1, 0, 0)
+        product_pass(early[1], 1, 0, 1)
+        quantise_x(1, HALF, HALF)
+        product_pass(late[0], 0, 1, 1)
+        product_pass(late[1], 1, 1, 1)
+        finish(late[0], 0, 1)
+        finish(late[1], 1, 1)
+        finish(early[0], 0, 0)
+        finish(early[1], 1, 0)

@@ -21,17 +21,22 @@ PASSES = 2
 BLOCKS = V // P
 HALF = V // 2
 BIAS_ROW = D
-CHUNKS = [[512, 512, 512, 256, 256], [768, 768, 512], [256, 768, 1024], [256, 1024, 768]]
-SHARES = [None, [384, 128, 256], [256, 256, 512], [256, 128, 0]]
+CHUNKS = [[512, 512, 512, 384, 128], [640, 640, 384, 384], [512, 384, 640, 512], [256, 1024, 512, 256]]
+SHARES = [None, [512, 0, 128, 0], [0, 0, 128, 0], [0, 256, 128, 0]]
 DIRECT = 3
 FUSED = []
-LAST = [2, 2]
+LAST = [3, 2]
 W_AFTER = 3
-PICKED = 3
-DIRECT_TAG = ['raw1_2', 'raw3_1']
+PICKED = 6
+DIRECT_TAG = ['raw2_0', 'raw3_3']
 HOLD = True
-MARK = (3, 0, 2)
+MARK = (3, 2, 2)
 W_TAG = 'mark'
+COUNT = [[8, 8, 8, 8], [6, 6, 6, 6]]
+LAST_ENGINES = ['scalar', 'scalar']
+FLIPS = 3
+WHOLE = [(0, 2, 0), (2, 0, 0)]
+MERGED = [(2, 0), (1, 2)]
 
 
 def tile_picked_bag_lin_gelu_sub_l_kernel(tc, xT, w, b, gate, offs, out):
@@ -80,11 +85,11 @@ def tile_picked_bag_lin_gelu_sub_l_kernel(tc, xT, w, b, gate, offs, out):
         nc.vector.memset(scratch[:], 0.0)
         nc.scalar.activation(scratch[:, 1:2], scratch[:, 0:1], ACT.Gelu_apprx_tanh)
         make_identity(nc, ident[:])
-        turned = psum.tile([P, BLOCKS, P], F32, tag="flip", name="turned")
+        turned = psum.tile([P, BLOCKS, P], F32, tag="flip", bufs=FLIPS, name="turned")
         for j in range(BLOCKS):
             nc.tensor.transpose(turned[:, j, :], rows[:, j * P : (j + 1) * P], ident[:])
         nc.scalar.copy(cols[:], turned[:, :, 0:8])
-        spread = psum.tile([P, V], F32, tag="flip", name="spread")
+        spread = psum.tile([P, V], F32, tag="flip", bufs=FLIPS, name="spread")
         for j in range(BLOCKS):
             nc.tensor.transpose(
                 spread[:, j * P : (j + 1) * P], cols[:, j, DIRECT : DIRECT + 1].to_broadcast([P, P]), ident[:]
@@ -111,10 +116,10 @@ def tile_picked_bag_lin_gelu_sub_l_kernel(tc, xT, w, b, gate, offs, out):
         held = {}
         direct = {}
 
-        def look_up_direct(q):
-            picked = keep.tile([P, V], U32, name="held%d" % q)
+        def look_up_direct(q, width):
+            picked = keep.tile([P, width], U32, name="held%d" % q)
             first = DIRECT * V // 16
-            nc.vector.tensor_copy(picked[:], windows[q][:].indirect(offsets[:, first : first + V // 16]))
+            nc.vector.tensor_copy(picked[:], windows[q][:].indirect(offsets[:, first : first + width // 16]))
             held[q] = picked
 
         def weigh_direct(q, start, width):
@@ -133,7 +138,7 @@ def tile_picked_bag_lin_gelu_sub_l_kernel(tc, xT, w, b, gate, offs, out):
         products = {}
 
         def weigh(q, d, j, bank, slot, engine):
-            product = ring.tile([P, 2, P], F32, tag="product", bufs=40, name="product")
+            product = ring.tile([P, 2, P], F32, tag="product", bufs=24, name="product")
             values = bank[:, slot, :].bitcast(BF16).rearrange("e (p i) -> e i p", i=2)
             if engine == "scalar":
                 nc.scalar.activation(product[:], values, ACT.Copy, scale=cols[:, j, d : d + 1])
@@ -146,6 +151,19 @@ def tile_picked_bag_lin_gelu_sub_l_kernel(tc, xT, w, b, gate, offs, out):
             products[q, d, j] = product
 
         banks = {}
+        second = {}
+
+        def weigh_whole(q, d, blocks):
+            n = len(blocks)
+            product = ring.tile([P, n, 2, P], F32, tag="whole", bufs=3, name="whole")
+            nc.vector.tensor_tensor(
+                product[:],
+                banks[q, d][:].bitcast(BF16).rearrange("e s (p i) -> e s i p", i=2),
+                cols[:, blocks[0] : blocks[0] + n, d : d + 1].unsqueeze(3).to_broadcast([P, n, 2, P]),
+                MULT,
+            )
+            for s, j in enumerate(blocks):
+                products[q, d, j] = product[:, s, :, :]
 
         def weigh_bank(q, d, blocks, engine):
             for s, j in enumerate(blocks):
@@ -154,40 +172,91 @@ def tile_picked_bag_lin_gelu_sub_l_kernel(tc, xT, w, b, gate, offs, out):
         def look_up(q, d, blocks, split):
             count = len(blocks) * P
             first = (d * V + blocks[0] * P) // 16
-            if (q, d, blocks[0]) == MARK:
-                picked = keep.tile([P, count], U32, tag="mark", name="picked", align_bytes=64)
+            if (q, d - 1) in MERGED:
+                words = second[q, d - 1]
+            elif (q, d) in MERGED:
+                picked = ring.tile([P, 2 * V], U32, tag="wide", bufs=2, name="picked")
+                nc.vector.tensor_copy(picked[:], windows[q][:].indirect(offsets[:, first : first + 2 * V // 16]))
+                words = picked[:, 0:V].bitcast(F32)
+                second[q, d] = picked[:, V : 2 * V].bitcast(F32)
             else:
-                picked = ring.tile([P, count], U32, tag="picked", bufs=PICKED, name="picked")
-            nc.vector.tensor_copy(picked[:], windows[q][:].indirect(offsets[:, first : first + count // 16]))
-            words = picked[:].bitcast(F32)
+                if (q, d, blocks[0]) == MARK:
+                    picked = keep.tile([P, count], U32, tag="mark", name="picked", align_bytes=64)
+                else:
+                    picked = ring.tile([P, count], U32, tag="picked", bufs=PICKED, name="picked")
+                nc.vector.tensor_copy(picked[:], windows[q][:].indirect(offsets[:, first : first + count // 16]))
+                words = picked[:].bitcast(F32)
             if split:
                 for s, j in enumerate(blocks):
-                    bank = psum.tile([P, 1, P], F32, tag="flip", name="flip")
+                    bank = psum.tile([P, 1, P], F32, tag="flip", bufs=FLIPS, name="flip")
                     nc.tensor.transpose(bank[:, 0, :], words[:, s * P : (s + 1) * P], ident[:])
-                    weigh(q, d, j, bank, 0, "scalar" if s == 0 else "vector")
+                    weigh(q, d, j, bank, 0, LAST_ENGINES[s])
             else:
-                bank = psum.tile([P, len(blocks), P], F32, tag="flip", name="flip")
+                bank = psum.tile([P, len(blocks), P], F32, tag="flip", bufs=FLIPS, name="flip")
                 for s, j in enumerate(blocks):
                     nc.tensor.transpose(bank[:, s, :], words[:, s * P : (s + 1) * P], ident[:])
                 banks[q, d] = bank
-                if (q, d) not in FUSED:
+                if (q, d) not in FUSED and (q, d, blocks[0]) not in WHOLE:
                     weigh_bank(q, d, blocks, "scalar")
 
+        early_words = {}
+
+        def look_up_early(ds):
+            count = len(ds) * V
+            first = ds[0] * V // 16
+            picked = keep.tile([P, count], U32, name="early_words%d" % ds[0])
+            nc.vector.tensor_copy(picked[:], windows[2][:].indirect(offsets[:, first : first + count // 16]))
+            for s, d in enumerate(ds):
+                early_words[d] = picked[:, s * V : (s + 1) * V].bitcast(F32)
+
+        def look_up_joint(d, blocks, engines):
+            first = (d * V + blocks[0] * P) // 16
+            if (3, d, blocks[0]) == MARK:
+                picked = keep.tile([P, HALF], U32, tag="mark", name="picked", align_bytes=64)
+            else:
+                picked = ring.tile([P, HALF], U32, tag="picked", bufs=PICKED, name="picked")
+            nc.vector.tensor_copy(picked[:], windows[3][:].indirect(offsets[:, first : first + HALF // 16]))
+            words = picked[:].bitcast(F32)
+            split = engines[0] != engines[1]
+            for s, j in enumerate(blocks):
+                if s == 0 or split:
+                    bank = psum.tile([P, 1 if split else 2, 2, P], F32, tag="flip", bufs=FLIPS, name="flip")
+                slot = 0 if split else s
+                nc.tensor.transpose(bank[:, slot, 0, :], early_words[d][:, j * P : (j + 1) * P], ident[:])
+                nc.tensor.transpose(bank[:, slot, 1, :], words[:, s * P : (s + 1) * P], ident[:])
+                banks[d, j, "joint"] = bank[:, slot, :, :]
+            if engines[0] == "scalar":
+                weigh_joint(d, blocks, engines, "scalar")
+
+        def weigh_joint(d, blocks, engines, only):
+            for s, j in enumerate(blocks):
+                if engines[s] == only:
+                    product = ring.tile([P, 2, 2, P], F32, tag="joint", bufs=8, name="product")
+                    values = banks[d, j, "joint"].bitcast(BF16).rearrange("e u (p i) -> e u i p", i=2)
+                    if only == "scalar":
+                        nc.scalar.activation(product[:], values, ACT.Copy, scale=cols[:, j, d : d + 1])
+                    else:
+                        nc.vector.tensor_scalar(product[:], values, cols[:, j, d : d + 1], None, MULT)
+                    products[2, d, j] = product[:, 0, :, :]
+                    products[3, d, j] = product[:, 1, :, :]
+
         sums = {}
+        added = {}
 
         def add_up(q, d, blocks):
             g, u = divmod(q, 2)
             for j in blocks:
                 fresh = (g, j) not in sums
+                added[g, j] = added.get((g, j), 0) + 1
                 if fresh:
-                    sums[g, j] = psum.tile([P, 4, P], F32, tag="acc", name="acc")
+                    sums[g, j] = psum.tile([P, 4, P], F32, tag="acc", bufs=8 - FLIPS, name="acc")
                 for i in range(2):
                     nc.tensor.matmul(
                         sums[g, j][:, 2 * u + i, :],
                         products[q, d, j][:, i, :],
                         ident[:],
                         start=(fresh and i == 0),
-                        stop=(u == 1 and d == LAST[g] and i == 1),
+                        stop=(added[g, j] == COUNT[g][j] and i == 1),
                         is_transpose=True,
                     )
 
@@ -259,86 +328,94 @@ def tile_picked_bag_lin_gelu_sub_l_kernel(tc, xT, w, b, gate, offs, out):
         cast(0, 4)
         cast_shared(1, 0, "pool")
         cast_shared(1, 0, "scalar")
+        cast_shared(1, 1, "pool")
         cast_shared(1, 1, "scalar")
+        cast_shared(1, 2, "pool")
+        cast_shared(1, 2, "scalar")
         cast_shared(2, 0, "pool")
         cast_shared(2, 0, "scalar")
+        cast_shared(2, 1, "pool")
         cast_shared(2, 1, "scalar")
+        cast_shared(2, 2, "pool")
+        cast_shared(2, 2, "scalar")
         look_up(0, 0, [0, 1, 2, 3], False)
-        cast_shared(1, 1, "pool")
-        cast_shared(1, 2, "scalar")
-        cast_shared(3, 0, "pool")
+        cast_shared(1, 3, "pool")
+        cast_shared(2, 3, "scalar")
+        cast_shared(3, 0, "scalar")
         look_up(0, 1, [0, 1, 2, 3], False)
         add_up(0, 0, [0, 1, 2, 3])
         look_up(0, 2, [0, 1, 2, 3], False)
         add_up(0, 1, [0, 1, 2, 3])
-        cast_shared(1, 2, "pool")
-        cast_shared(3, 1, "pool")
-        look_up_direct(0)
-        weigh_direct(0, 0, V)
+        cast_shared(1, 3, "scalar")
+        cast_shared(3, 1, "scalar")
+        look_up(0, 3, [0, 1, 2, 3], False)
+        weigh_whole(0, 2, [0, 1, 2, 3])
         add_up(0, 2, [0, 1, 2, 3])
-        cast_shared(2, 1, "pool")
-        cast_shared(2, 2, "scalar")
+        cast_shared(2, 3, "pool")
+        cast_shared(3, 0, "pool")
+        cast_shared(3, 2, "scalar")
         look_up(1, 0, [0, 1, 2, 3], False)
-        cast_shared(2, 2, "pool")
+        add_up(0, 3, [0, 1, 2, 3])
         look_up(1, 1, [0, 1, 2, 3], False)
         add_up(1, 0, [0, 1, 2, 3])
-        cast_shared(3, 0, "scalar")
         look_up(1, 2, [0, 1, 2, 3], False)
         add_up(1, 1, [0, 1, 2, 3])
-        cast_shared(3, 1, "scalar")
-        look_up_direct(1)
-        weigh_direct(1, 0, V)
+        look_up(1, 3, [0, 1, 2, 3], False)
         add_up(1, 2, [0, 1, 2, 3])
+        cast_shared(3, 1, "pool")
         cast_w(1, "pool")
         look_up(2, 0, [0, 1, 2, 3], False)
-        look_up(2, 1, [0, 1, 2, 3], False)
-        cast_shared(3, 2, "scalar")
-        look_up(2, 2, [0, 1, 2, 3], False)
-        round_sums(0, 0)
-        round_sums(0, 1)
+        add_up(1, 3, [0, 1, 2, 3])
+        round_plain(0, 0, "scalar")
         cast_shared(3, 2, "pool")
-        look_up_direct(2)
+        cast_shared(3, 3, "scalar")
+        look_up(2, 1, [0, 1, 2, 3], False)
+        look_up_direct(2, V)
         weigh_direct(2, 0, V)
-        round_sums(0, 2)
-        round_sums(0, 3)
         cast_w(0, "pool")
-        look_up_direct(3)
-        weigh_direct(3, 0, HALF)
-        weigh_direct(3, HALF, HALF)
+        look_up(2, 2, [0, 1, 2, 3], False)
+        round_plain(0, 1, "vector")
+        cast_shared(3, 3, "pool")
+        look_up(3, 0, [0, 1], False)
+        round_plain(0, 2, "vector")
+        round_plain(0, 3, "scalar")
+        quantise_x(0, 0, V)
+        look_up(3, 1, [0, 1], False)
+        weigh_whole(2, 0, [0, 1, 2, 3])
         add_up(2, 0, [0, 1, 2, 3])
         add_up(2, 1, [0, 1, 2, 3])
         add_up(2, 2, [0, 1, 2, 3])
-        look_up(3, 0, [0, 1], False)
-        look_up(3, 1, [0, 1], False)
         add_up(3, 0, [0, 1])
-        quantise_x(0, 0, V)
         look_up(3, 2, [0, 1], False)
         add_up(3, 1, [0, 1])
-        look_up(3, 0, [2, 3], False)
+        look_up_direct(3, V)
+        weigh_direct(3, 0, HALF)
+        weigh_direct(3, HALF, HALF)
         add_up(3, 2, [0, 1])
         round_sums(1, 0)
+        look_up(3, 0, [2, 3], False)
+        round_sums(1, 1)
         look_up(3, 1, [2, 3], False)
         add_up(3, 0, [2, 3])
-        quantise_w()
         look_up(3, 2, [2, 3], True)
         add_up(3, 1, [2, 3])
-        round_sums(1, 1)
+        quantise_w()
         add_up(3, 2, [2, 3])
-        late = [psum.tile([P, HALF], F32, tag="flip", name="late") for m in range(2)]
-        early = [psum.tile([P, HALF], F32, tag="acc", name="early") for m in range(2)]
+        late = [psum.tile([P, HALF], F32, tag="flip", bufs=FLIPS, name="late") for m in range(2)]
+        early = [psum.tile([P, HALF], F32, tag="acc", bufs=8 - FLIPS, name="early") for m in range(2)]
         quantise_x(1, 0, HALF)
-        round_sums(1, 3)
-        round_sums(1, 2)
         product_pass(late[0], 0, 1, 0)
         product_pass(late[1], 1, 1, 0)
         product_pass(early[0], 0, 0, 0)
         product_pass(early[0], 0, 0, 1)
         product_pass(early[1], 1, 0, 0)
         product_pass(early[1], 1, 0, 1)
+        round_sums(1, 2)
+        round_sums(1, 3)
+        finish(early[0], 0, 0)
+        finish(early[1], 1, 0)
         quantise_x(1, HALF, HALF)
         product_pass(late[0], 0, 1, 1)
         product_pass(late[1], 1, 1, 1)
         finish(late[0], 0, 1)
         finish(late[1], 1, 1)
-        finish(early[0], 0, 0)
-        finish(early[1], 1, 0)

@@ -17,26 +17,22 @@ MULT = mybir.AluOpType.mult
 ADD = mybir.AluOpType.add
 
 P = 128
-PASSES = 2
-BLOCKS = V // P
+PACK = 4
+K_PASS = P * PACK
+PASSES = K // K_PASS
+WINDOWS = 2 * PASSES
+GROUPS = V // P
 HALF = V // 2
+LIST_ROWS = 16
 BIAS_ROW = D
-CHUNKS = [[512, 512, 512, 384, 128], [640, 640, 384, 384], [512, 384, 640, 512], [256, 1024, 512, 256]]
-SHARES = [None, [512, 0, 128, 0], [0, 0, 128, 0], [0, 256, 128, 0]]
-DIRECT = 3
-FUSED = []
-LAST = [3, 2]
-W_AFTER = 3
-PICKED = 6
-DIRECT_TAG = ['raw2_0', 'raw3_3']
-HOLD = True
-MARK = (3, 2, 2)
-W_TAG = 'mark'
-COUNT = [[8, 8, 8, 8], [6, 6, 6, 6]]
-LAST_ENGINES = ['scalar', 'scalar']
-FLIPS = 3
-WHOLE = [(0, 2, 0), (2, 0, 0)]
-MERGED = [(2, 0), (1, 2)]
+COLUMNS_KEPT = 8
+DIRECT = D - 1
+
+CHUNKS = [[1024, 640, 384], [768, 640, 640], [768, 768, 512], [768, 640, 640]]
+SCALAR_COLUMNS = [[0, 0, 0], [384, 128, 0], [0, 256, 0], [0, 128, 128]]
+TURN_BANKS, SUM_BANKS = 3, 5
+PICKED_BUFS = 4
+PRODUCT_BUFS = 24
 
 
 def tile_picked_bag_lin_gelu_sub_l_kernel(tc, xT, w, b, gate, offs, out):
@@ -44,255 +40,125 @@ def tile_picked_bag_lin_gelu_sub_l_kernel(tc, xT, w, b, gate, offs, out):
     with ExitStack() as ctx:
         keep = ctx.enter_context(tc.tile_pool(name="keep", bufs=1))
         ring = ctx.enter_context(tc.tile_pool(name="ring", bufs=1))
-        psum = ctx.enter_context(tc.psum_pool(name="psum", bufs=4))
+        psum = ctx.enter_context(tc.psum_pool(name="psum", bufs=1))
 
-        offsets = keep.tile([P, D * V // 16], U16, name="offsets")
+        offsets = keep.tile([P, D * V // LIST_ROWS], U16, name="offsets")
         ident = keep.tile([P, P], F32, name="ident")
         rows = keep.tile([P, V], F32, name="rows")
-        cols = keep.tile([P, BLOCKS, 8], F32, name="cols")
+        cols = keep.tile([P, GROUPS, COLUMNS_KEPT], F32, name="cols")
         scratch = keep.tile([P, 8], F32, name="scratch")
-        windows = [keep.tile([P, T], U32, name="window%d" % q) for q in range(4)]
-        w_raw = keep.tile([P, PASSES, 4, N], F32, name="w_raw")
-        w_bf = keep.tile([P, PASSES, N, 4], BF16, name="w_bf", align_bytes=64)
+        windows = [keep.tile([P, T], U32, name="window%d" % q) for q in range(WINDOWS)]
+        w_raw = keep.tile([P, PASSES, PACK, N], F32, name="w_raw")
+        w_bf = keep.tile([P, PASSES, N, PACK], BF16, name="w_bf", align_bytes=64)
         w_scales = keep.tile([P, PASSES * N], U8, name="w_scales", align_bytes=64)
-        x_bf = [keep.tile([P, V, 4], BF16, name="x_bf%d" % g, align_bytes=64) for g in range(PASSES)]
+        x_bf = [keep.tile([P, V, PACK], BF16, name="x_bf%d" % g, align_bytes=64) for g in range(PASSES)]
         x_codes = [keep.tile([P, V], U32, name="x_codes%d" % g, align_bytes=64) for g in range(PASSES)]
         x_scales = [keep.tile([P, V], U8, name="x_scales%d" % g, align_bytes=64) for g in range(PASSES)]
-
         gate_pairs = keep.tile([P, V, 2], F32, name="gate_pairs")
 
         nc.gpsimd.memset(rows[:], 0.0)
         raw = {}
-        for q in range(4):
+        for q in range(WINDOWS):
             g, u = divmod(q, 2)
-            src = xT[g * 512 : (g + 1) * 512, :].rearrange("(p j) t -> p j t", j=4)
+            pass_rows = xT[g * K_PASS : (g + 1) * K_PASS, :].rearrange("(p t) c -> p t c", t=PACK)
             start = 0
             for c, width in enumerate(CHUNKS[q]):
                 chunk = keep.tile([P, 2, width], F32, name="raw%d_%d" % (q, c))
-                nc.sync.dma_start(out=chunk[:], in_=src[:, 2 * u : 2 * u + 2, start : start + width])
-                raw[q, c] = (chunk, start, width)
+                nc.sync.dma_start(out=chunk[:], in_=pass_rows[:, 2 * u : 2 * u + 2, start : start + width])
+                raw[q, c] = (chunk, start)
                 start += width
                 if (q, c) == (0, 0):
                     nc.sync.dma_start(out=rows[0:D, :], in_=gate[:, 0, :])
                     nc.sync.dma_start(out=rows[BIAS_ROW : BIAS_ROW + 1, 0:N], in_=b.rearrange("n o -> o n"))
                     nc.sync.dma_start(offsets[:], offs)
-            if q == W_AFTER:
-                for g in range(PASSES):
-                    nc.sync.dma_start(
-                        out=w_raw[:, g, :, :], in_=w[g * 512 : (g + 1) * 512, :].rearrange("(p j) n -> p j n", j=4)
-                    )
+        for g in range(PASSES):
+            nc.sync.dma_start(
+                out=w_raw[:, g, :, :], in_=w[g * K_PASS : (g + 1) * K_PASS, :].rearrange("(p t) n -> p t n", t=PACK)
+            )
 
         nc.vector.memset(scratch[:], 0.0)
         nc.scalar.activation(scratch[:, 1:2], scratch[:, 0:1], ACT.Gelu_apprx_tanh)
+
         make_identity(nc, ident[:])
-        turned = psum.tile([P, BLOCKS, P], F32, tag="flip", bufs=FLIPS, name="turned")
-        for j in range(BLOCKS):
+        turned = psum.tile([P, GROUPS, P], F32, tag="turn", bufs=TURN_BANKS, name="turned")
+        for j in range(GROUPS):
             nc.tensor.transpose(turned[:, j, :], rows[:, j * P : (j + 1) * P], ident[:])
-        nc.scalar.copy(cols[:], turned[:, :, 0:8])
-        spread = psum.tile([P, V], F32, tag="flip", bufs=FLIPS, name="spread")
-        for j in range(BLOCKS):
+        nc.scalar.copy(cols[:], turned[:, :, 0:COLUMNS_KEPT])
+        spread = psum.tile([P, V], F32, tag="turn", bufs=TURN_BANKS, name="spread")
+        for j in range(GROUPS):
             nc.tensor.transpose(
                 spread[:, j * P : (j + 1) * P], cols[:, j, DIRECT : DIRECT + 1].to_broadcast([P, P]), ident[:]
             )
         nc.scalar.copy(gate_pairs[:], spread[:].unsqueeze(2).to_broadcast([P, V, 2]))
 
-        def cast(q, c):
-            chunk, start, width = raw[q, c]
-            pairs = windows[q][:, start : start + width].bitcast(BF16).rearrange("p (t i) -> p t i", i=2)
-            nc.vector.tensor_copy(out=pairs, in_=chunk[:].rearrange("p i t -> p t i"))
+        def cast_operands(q, c, first, last):
+            chunk, start = raw[q, c]
+            pairs = windows[q][:, start + first : start + last].bitcast(BF16).rearrange("p (c i) -> p c i", i=2)
+            return pairs, chunk[:, :, first:last].rearrange("p i c -> p c i")
 
-        def cast_shared(q, c, engine):
-            chunk, start, width = raw[q, c]
-            share = SHARES[q][c]
-            a, z = (0, share) if engine == "scalar" else (share, width)
-            if z > a:
-                pairs = windows[q][:, start + a : start + z].bitcast(BF16).rearrange("p (t i) -> p t i", i=2)
-                values = chunk[:, :, a:z].rearrange("p i t -> p t i")
-                if engine == "scalar":
-                    nc.scalar.copy(pairs, values)
-                else:
-                    nc.gpsimd.tensor_scalar(pairs, values, 1.0, 0.0, MULT, ADD)
+        def cast_w(g):
+            nc.gpsimd.tensor_scalar(w_bf[:, g, :, :], w_raw[:, g, :, :].rearrange("p t n -> p n t"), 1.0, 0.0, MULT, ADD)
 
-        held = {}
-        direct = {}
-
-        def look_up_direct(q, width):
-            picked = keep.tile([P, width], U32, name="held%d" % q)
-            first = DIRECT * V // 16
-            nc.vector.tensor_copy(picked[:], windows[q][:].indirect(offsets[:, first : first + width // 16]))
-            held[q] = picked
-
-        def weigh_direct(q, start, width):
-            g, u = divmod(q, 2)
-            if g not in direct:
-                direct[g] = keep.tile([P, 2, V, 2], F32, name="direct%d" % g, tag=DIRECT_TAG[g])
-            if q == 1 and HOLD:
-                nc.gpsimd.tensor_copy(direct[g][:, u, 0, :], windows[2][:, T - 1 : T].bitcast(BF16))
-            nc.gpsimd.tensor_tensor(
-                direct[g][:, u, start : start + width, :].rearrange("p v i -> p (v i)"),
-                held[q][:, start : start + width].bitcast(BF16),
-                gate_pairs[:, start : start + width, :].rearrange("p v i -> p (v i)"),
-                MULT,
-            )
+        def gather(picked, q, entry, count):
+            entries = offsets[:, entry // LIST_ROWS : (entry + count) // LIST_ROWS]
+            nc.vector.tensor_copy(picked[:], windows[q][:].indirect(entries))
 
         products = {}
 
-        def weigh(q, d, j, bank, slot, engine):
-            product = ring.tile([P, 2, P], F32, tag="product", bufs=24, name="product")
-            values = bank[:, slot, :].bitcast(BF16).rearrange("e (p i) -> e i p", i=2)
-            if engine == "scalar":
-                nc.scalar.activation(product[:], values, ACT.Copy, scale=cols[:, j, d : d + 1])
-            elif engine == "fused":
-                nc.vector.scalar_tensor_tensor(
-                    product[:], values, cols[:, j, d : d + 1], products.pop((q, d - 1, j))[:], MULT, ADD
-                )
-            else:
-                nc.vector.tensor_scalar(product[:], values, cols[:, j, d : d + 1], None, MULT)
+        def weigh(q, d, j, words):
+            product = ring.tile([P, 2, P], F32, tag="product", bufs=PRODUCT_BUFS, name="product")
+            values = words.bitcast(BF16).rearrange("e (p i) -> e i p", i=2)
+            nc.scalar.activation(product[:], values, ACT.Copy, scale=cols[:, j, d : d + 1])
             products[q, d, j] = product
 
-        banks = {}
-        second = {}
+        def turn_and_weigh(q, d, groups, picked):
+            bank = psum.tile([P, len(groups), P], F32, tag="turn", bufs=TURN_BANKS, name="turn")
+            for s in range(len(groups)):
+                nc.tensor.transpose(bank[:, s, :], picked.bitcast(F32)[:, s * P : (s + 1) * P], ident[:])
+            for s, j in enumerate(groups):
+                weigh(q, d, j, bank[:, s, :])
 
-        def weigh_whole(q, d, blocks):
-            n = len(blocks)
-            product = ring.tile([P, n, 2, P], F32, tag="whole", bufs=3, name="whole")
-            nc.vector.tensor_tensor(
-                product[:],
-                banks[q, d][:].bitcast(BF16).rearrange("e s (p i) -> e s i p", i=2),
-                cols[:, blocks[0] : blocks[0] + n, d : d + 1].unsqueeze(3).to_broadcast([P, n, 2, P]),
-                MULT,
-            )
-            for s, j in enumerate(blocks):
-                products[q, d, j] = product[:, s, :, :]
-
-        def weigh_bank(q, d, blocks, engine):
-            for s, j in enumerate(blocks):
-                weigh(q, d, j, banks[q, d], s, engine)
-
-        def look_up(q, d, blocks, split):
-            count = len(blocks) * P
-            first = (d * V + blocks[0] * P) // 16
-            if (q, d - 1) in MERGED:
-                words = second[q, d - 1]
-            elif (q, d) in MERGED:
-                picked = ring.tile([P, 2 * V], U32, tag="wide", bufs=2, name="picked")
-                nc.vector.tensor_copy(picked[:], windows[q][:].indirect(offsets[:, first : first + 2 * V // 16]))
-                words = picked[:, 0:V].bitcast(F32)
-                second[q, d] = picked[:, V : 2 * V].bitcast(F32)
-            else:
-                if (q, d, blocks[0]) == MARK:
-                    picked = keep.tile([P, count], U32, tag="mark", name="picked", align_bytes=64)
-                else:
-                    picked = ring.tile([P, count], U32, tag="picked", bufs=PICKED, name="picked")
-                nc.vector.tensor_copy(picked[:], windows[q][:].indirect(offsets[:, first : first + count // 16]))
-                words = picked[:].bitcast(F32)
-            if split:
-                for s, j in enumerate(blocks):
-                    bank = psum.tile([P, 1, P], F32, tag="flip", bufs=FLIPS, name="flip")
-                    nc.tensor.transpose(bank[:, 0, :], words[:, s * P : (s + 1) * P], ident[:])
-                    weigh(q, d, j, bank, 0, LAST_ENGINES[s])
-            else:
-                bank = psum.tile([P, len(blocks), P], F32, tag="flip", bufs=FLIPS, name="flip")
-                for s, j in enumerate(blocks):
-                    nc.tensor.transpose(bank[:, s, :], words[:, s * P : (s + 1) * P], ident[:])
-                banks[q, d] = bank
-                if (q, d) not in FUSED and (q, d, blocks[0]) not in WHOLE:
-                    weigh_bank(q, d, blocks, "scalar")
-
-        early_words = {}
-
-        def look_up_early(ds):
-            count = len(ds) * V
-            first = ds[0] * V // 16
-            picked = keep.tile([P, count], U32, name="early_words%d" % ds[0])
-            nc.vector.tensor_copy(picked[:], windows[2][:].indirect(offsets[:, first : first + count // 16]))
-            for s, d in enumerate(ds):
-                early_words[d] = picked[:, s * V : (s + 1) * V].bitcast(F32)
-
-        def look_up_joint(d, blocks, engines):
-            first = (d * V + blocks[0] * P) // 16
-            if (3, d, blocks[0]) == MARK:
-                picked = keep.tile([P, HALF], U32, tag="mark", name="picked", align_bytes=64)
-            else:
-                picked = ring.tile([P, HALF], U32, tag="picked", bufs=PICKED, name="picked")
-            nc.vector.tensor_copy(picked[:], windows[3][:].indirect(offsets[:, first : first + HALF // 16]))
-            words = picked[:].bitcast(F32)
-            split = engines[0] != engines[1]
-            for s, j in enumerate(blocks):
-                if s == 0 or split:
-                    bank = psum.tile([P, 1 if split else 2, 2, P], F32, tag="flip", bufs=FLIPS, name="flip")
-                slot = 0 if split else s
-                nc.tensor.transpose(bank[:, slot, 0, :], early_words[d][:, j * P : (j + 1) * P], ident[:])
-                nc.tensor.transpose(bank[:, slot, 1, :], words[:, s * P : (s + 1) * P], ident[:])
-                banks[d, j, "joint"] = bank[:, slot, :, :]
-            if engines[0] == "scalar":
-                weigh_joint(d, blocks, engines, "scalar")
-
-        def weigh_joint(d, blocks, engines, only):
-            for s, j in enumerate(blocks):
-                if engines[s] == only:
-                    product = ring.tile([P, 2, 2, P], F32, tag="joint", bufs=8, name="product")
-                    values = banks[d, j, "joint"].bitcast(BF16).rearrange("e u (p i) -> e u i p", i=2)
-                    if only == "scalar":
-                        nc.scalar.activation(product[:], values, ACT.Copy, scale=cols[:, j, d : d + 1])
-                    else:
-                        nc.vector.tensor_scalar(product[:], values, cols[:, j, d : d + 1], None, MULT)
-                    products[2, d, j] = product[:, 0, :, :]
-                    products[3, d, j] = product[:, 1, :, :]
+        def look_up(q, d, groups):
+            picked = ring.tile([P, len(groups) * P], U32, tag="picked", bufs=PICKED_BUFS, name="picked")
+            gather(picked, q, d * V + groups[0] * P, len(groups) * P)
+            turn_and_weigh(q, d, groups, picked[:])
 
         sums = {}
-        added = {}
 
-        def add_up(q, d, blocks):
+        def add_up(q, d, groups):
             g, u = divmod(q, 2)
-            for j in blocks:
-                fresh = (g, j) not in sums
-                added[g, j] = added.get((g, j), 0) + 1
-                if fresh:
-                    sums[g, j] = psum.tile([P, 4, P], F32, tag="acc", bufs=8 - FLIPS, name="acc")
+            last_turned = D - 1 if g == 0 else DIRECT - 1
+            for j in groups:
+                if (u, d) == (0, 0):
+                    sums[g, j] = psum.tile([P, PACK, P], F32, tag="sum", bufs=SUM_BANKS, name="sums")
                 for i in range(2):
                     nc.tensor.matmul(
                         sums[g, j][:, 2 * u + i, :],
                         products[q, d, j][:, i, :],
                         ident[:],
-                        start=(fresh and i == 0),
-                        stop=(added[g, j] == COUNT[g][j] and i == 1),
+                        start=((u, d, i) == (0, 0, 0)),
+                        stop=((u, d, i) == (1, last_turned, 1)),
                         is_transpose=True,
                     )
 
-        def round_plain(g, j, engine):
-            dst = x_bf[g][:, j * P : (j + 1) * P, :]
-            src = sums[g, j][:].rearrange("p t c -> p c t")
-            if engine == "scalar":
-                nc.scalar.copy(dst, src)
-            else:
-                nc.vector.tensor_copy(dst, src)
-
-        late_tiles = {}
-
-        def quantise_w():
-            w_codes = keep.tile([P, PASSES * N], U32, name="w_codes", align_bytes=64, tag=W_TAG)
-            late_tiles["w"] = w_codes
-            nc.vector.quantize_mx(
-                out=w_codes[:].bitcast(FP8X4),
-                scales=w_scales[:],
-                in_=w_bf[:].rearrange("p g n j -> p (g n j)"),
+        def weigh_direct(direct, u, picked, start, width):
+            nc.gpsimd.tensor_tensor(
+                direct[:, u, start : start + width, :].rearrange("p v i -> p (v i)"),
+                picked[:, start : start + width].bitcast(BF16),
+                gate_pairs[:, start : start + width, :].rearrange("p v i -> p (v i)"),
+                MULT,
             )
 
-        def round_sums(g, j):
+        def round_pass0(j, copy):
+            copy(x_bf[0][:, j * P : (j + 1) * P, :], sums[0, j][:].rearrange("p t c -> p c t"))
+
+        def round_pass1(j, direct):
             nc.vector.tensor_tensor(
-                x_bf[g][:, j * P : (j + 1) * P, :].rearrange("p c (u i) -> p c u i", i=2),
-                sums[g, j][:].rearrange("p (u i) c -> p c u i", i=2),
-                direct[g][:, :, j * P : (j + 1) * P, :].rearrange("p u c i -> p c u i"),
+                x_bf[1][:, j * P : (j + 1) * P, :].rearrange("p c (u i) -> p c u i", i=2),
+                sums[1, j][:].rearrange("p (u i) c -> p c u i", i=2),
+                direct[:, :, j * P : (j + 1) * P, :].rearrange("p u c i -> p c u i"),
                 ADD,
             )
-
-        def cast_w(g, engine):
-            values = w_raw[:, g, :, :].rearrange("p j n -> p n j")
-            if engine == "scalar":
-                nc.scalar.copy(w_bf[:, g, :, :], values)
-            else:
-                nc.gpsimd.tensor_scalar(w_bf[:, g, :, :], values, 1.0, 0.0, MULT, ADD)
 
         def quantise_x(g, start, width):
             nc.vector.quantize_mx(
@@ -301,121 +167,101 @@ def tile_picked_bag_lin_gelu_sub_l_kernel(tc, xT, w, b, gate, offs, out):
                 in_=x_bf[g][:, start : start + width, :].rearrange("p v t -> p (v t)"),
             )
 
-        def product_pass(acc, m, h, g):
-            wc = slice(g * N + m * P, g * N + (m + 1) * P)
-            xc = slice(h * HALF, (h + 1) * HALF)
+        def multiply(acc, w_codes, m, half, g):
+            w_cols = slice(g * N + m * P, g * N + (m + 1) * P)
+            x_cols = slice(half * HALF, (half + 1) * HALF)
             nc.tensor.matmul_mx(
                 out=acc[:],
-                lhsT=late_tiles["w"][:, wc].bitcast(FP8X4),
-                lhsT_scale=w_scales[:, wc],
-                rhs=x_codes[g][:, xc].bitcast(FP8X4),
-                rhs_scale=x_scales[g][:, xc],
+                lhsT=w_codes[:, w_cols].bitcast(FP8X4),
+                lhsT_scale=w_scales[:, w_cols],
+                rhs=x_codes[g][:, x_cols].bitcast(FP8X4),
+                rhs_scale=x_scales[g][:, x_cols],
                 start=(g == 0),
                 stop=(g == PASSES - 1),
             )
 
-        def finish(acc, m, h):
-            result = keep.tile([P, HALF], F32, name="result%d_%d" % (m, h))
-            nc.scalar.activation(
-                result[:], acc[:], ACT.Gelu_apprx_tanh, bias=cols[:, m, BIAS_ROW : BIAS_ROW + 1]
-            )
-            nc.sync.dma_start(out=out[m * P : (m + 1) * P, h * HALF : (h + 1) * HALF], in_=result[:])
+        def finish(acc, m, half):
+            result = keep.tile([P, HALF], F32, name="result%d_%d" % (m, half))
+            nc.scalar.activation(result[:], acc[:], ACT.Gelu_apprx_tanh, bias=cols[:, m, BIAS_ROW : BIAS_ROW + 1])
+            nc.sync.dma_start(out=out[m * P : (m + 1) * P, half * HALF : (half + 1) * HALF], in_=result[:])
 
-        cast(0, 0)
-        cast(0, 1)
-        cast(0, 2)
-        cast(0, 3)
-        cast(0, 4)
-        cast_shared(1, 0, "pool")
-        cast_shared(1, 0, "scalar")
-        cast_shared(1, 1, "pool")
-        cast_shared(1, 1, "scalar")
-        cast_shared(1, 2, "pool")
-        cast_shared(1, 2, "scalar")
-        cast_shared(2, 0, "pool")
-        cast_shared(2, 0, "scalar")
-        cast_shared(2, 1, "pool")
-        cast_shared(2, 1, "scalar")
-        cast_shared(2, 2, "pool")
-        cast_shared(2, 2, "scalar")
-        look_up(0, 0, [0, 1, 2, 3], False)
-        cast_shared(1, 3, "pool")
-        cast_shared(2, 3, "scalar")
-        cast_shared(3, 0, "scalar")
-        look_up(0, 1, [0, 1, 2, 3], False)
-        add_up(0, 0, [0, 1, 2, 3])
-        look_up(0, 2, [0, 1, 2, 3], False)
-        add_up(0, 1, [0, 1, 2, 3])
-        cast_shared(1, 3, "scalar")
-        cast_shared(3, 1, "scalar")
-        look_up(0, 3, [0, 1, 2, 3], False)
-        weigh_whole(0, 2, [0, 1, 2, 3])
-        add_up(0, 2, [0, 1, 2, 3])
-        cast_shared(2, 3, "pool")
-        cast_shared(3, 0, "pool")
-        cast_shared(3, 2, "scalar")
-        look_up(1, 0, [0, 1, 2, 3], False)
-        add_up(0, 3, [0, 1, 2, 3])
-        look_up(1, 1, [0, 1, 2, 3], False)
-        add_up(1, 0, [0, 1, 2, 3])
-        look_up(1, 2, [0, 1, 2, 3], False)
-        add_up(1, 1, [0, 1, 2, 3])
-        look_up(1, 3, [0, 1, 2, 3], False)
-        add_up(1, 2, [0, 1, 2, 3])
-        cast_shared(3, 1, "pool")
-        cast_w(1, "pool")
-        look_up(2, 0, [0, 1, 2, 3], False)
-        add_up(1, 3, [0, 1, 2, 3])
-        round_plain(0, 0, "scalar")
-        cast_shared(3, 2, "pool")
-        cast_shared(3, 3, "scalar")
-        look_up(2, 1, [0, 1, 2, 3], False)
-        look_up_direct(2, V)
-        weigh_direct(2, 0, V)
-        cast_w(0, "pool")
-        look_up(2, 2, [0, 1, 2, 3], False)
-        round_plain(0, 1, "vector")
-        cast_shared(3, 3, "pool")
-        look_up(3, 0, [0, 1], False)
-        round_plain(0, 2, "vector")
-        round_plain(0, 3, "scalar")
+        for c, width in enumerate(CHUNKS[0]):
+            nc.vector.tensor_copy(*cast_operands(0, c, 0, width))
+        for q in range(1, WINDOWS):
+            for c, width in enumerate(CHUNKS[q]):
+                split = SCALAR_COLUMNS[q][c]
+                nc.gpsimd.tensor_scalar(*cast_operands(q, c, split, width), 1.0, 0.0, MULT, ADD)
+                if split > 0:
+                    nc.scalar.copy(*cast_operands(q, c, 0, split))
+
+        every, low, high = list(range(GROUPS)), [0, 1], [2, 3]
+
+        pieces = [(q, d) for q in range(2) for d in range(D)]
+        for n, (q, d) in enumerate(pieces):
+            look_up(q, d, every)
+            if n > 0:
+                add_up(*pieces[n - 1], every)
+
+        two_pieces = keep.tile([P, 2 * V], U32, name="two_pieces")
+        gather(two_pieces, 2, 0, 2 * V)
+        turn_and_weigh(2, 0, every, two_pieces[:, 0:V])
+        add_up(*pieces[-1], every)
+        cast_w(1)
+        turn_and_weigh(2, 1, every, two_pieces[:, V : 2 * V])
+        held = [keep.tile([P, V], U32, name="held%d" % u) for u in range(2)]
+        gather(held[0], 2, DIRECT * V, V)
+        direct = keep.tile([P, 2, V, 2], F32, name="direct", tag="raw%d_%d" % (WINDOWS - 1, len(CHUNKS[-1]) - 1))
+        weigh_direct(direct, 0, held[0], 0, V)
+        round_pass0(0, nc.vector.tensor_copy)
+        look_up(2, 2, every)
+        round_pass0(1, nc.vector.tensor_copy)
+        cast_w(0)
+
+        look_up(3, 0, low)
+        round_pass0(2, nc.vector.tensor_copy)
+        round_pass0(3, nc.scalar.copy)
+        look_up(3, 1, low)
+        for d in range(DIRECT):
+            add_up(2, d, every)
+        add_up(3, 0, low)
+        gather(held[1], 3, DIRECT * V, V)
+        for half in range(2):
+            weigh_direct(direct, 1, held[1], half * HALF, HALF)
+        add_up(3, 1, low)
+        look_up(3, 2, low)
+        look_up(3, 0, high)
+        add_up(3, 2, low)
+        round_pass1(0, direct)
+        look_up(3, 1, high)
+        add_up(3, 0, high)
         quantise_x(0, 0, V)
-        look_up(3, 1, [0, 1], False)
-        weigh_whole(2, 0, [0, 1, 2, 3])
-        add_up(2, 0, [0, 1, 2, 3])
-        add_up(2, 1, [0, 1, 2, 3])
-        add_up(2, 2, [0, 1, 2, 3])
-        add_up(3, 0, [0, 1])
-        look_up(3, 2, [0, 1], False)
-        add_up(3, 1, [0, 1])
-        look_up_direct(3, V)
-        weigh_direct(3, 0, HALF)
-        weigh_direct(3, HALF, HALF)
-        add_up(3, 2, [0, 1])
-        round_sums(1, 0)
-        look_up(3, 0, [2, 3], False)
-        round_sums(1, 1)
-        look_up(3, 1, [2, 3], False)
-        add_up(3, 0, [2, 3])
-        look_up(3, 2, [2, 3], True)
-        add_up(3, 1, [2, 3])
-        quantise_w()
-        add_up(3, 2, [2, 3])
-        late = [psum.tile([P, HALF], F32, tag="flip", bufs=FLIPS, name="late") for m in range(2)]
-        early = [psum.tile([P, HALF], F32, tag="acc", bufs=8 - FLIPS, name="early") for m in range(2)]
+
+        last = keep.tile([P, HALF], U32, tag="last", name="last", align_bytes=64)
+        gather(last, 3, (DIRECT - 1) * V + HALF, HALF)
+        for s, j in enumerate(high):
+            turn_and_weigh(3, DIRECT - 1, [j], last[:, s * P : (s + 1) * P])
+        add_up(3, 1, high)
+        w_codes = keep.tile([P, PASSES * N], U32, tag="last", name="w_codes", align_bytes=64)
+        nc.vector.quantize_mx(
+            out=w_codes[:].bitcast(FP8X4), scales=w_scales[:], in_=w_bf[:].rearrange("p g n t -> p (g n t)")
+        )
+        round_pass1(1, direct)
+        add_up(3, DIRECT - 1, high)
+
+        acc_high = [psum.tile([P, HALF], F32, tag="turn", bufs=TURN_BANKS, name="acc_high") for m in range(N // P)]
+        acc_low = [psum.tile([P, HALF], F32, tag="sum", bufs=SUM_BANKS, name="acc_low") for m in range(N // P)]
         quantise_x(1, 0, HALF)
-        product_pass(late[0], 0, 1, 0)
-        product_pass(late[1], 1, 1, 0)
-        product_pass(early[0], 0, 0, 0)
-        product_pass(early[0], 0, 0, 1)
-        product_pass(early[1], 1, 0, 0)
-        product_pass(early[1], 1, 0, 1)
-        round_sums(1, 2)
-        round_sums(1, 3)
-        finish(early[0], 0, 0)
-        finish(early[1], 1, 0)
+        for m in range(N // P):
+            for g in range(PASSES):
+                multiply(acc_low[m], w_codes, m, 0, g)
+        for m in range(N // P):
+            multiply(acc_high[m], w_codes, m, 1, 0)
+        for j in high:
+            round_pass1(j, direct)
         quantise_x(1, HALF, HALF)
-        product_pass(late[0], 0, 1, 1)
-        product_pass(late[1], 1, 1, 1)
-        finish(late[0], 0, 1)
-        finish(late[1], 1, 1)
+        for m in range(N // P):
+            multiply(acc_high[m], w_codes, m, 1, 1)
+        for m in range(N // P):
+            finish(acc_high[m], m, 1)
+        for m in range(N // P):
+            finish(acc_low[m], m, 0)

from contextlib import ExitStack

import concourse.mybir as mybir
from concourse.masks import make_identity

K, T, D, V, N = 1024, 2048, 4, 512, 256
FLOPS = 2 * K * N * V

F32 = mybir.dt.float32
BF16 = mybir.dt.bfloat16
U32 = mybir.dt.uint32
U16 = mybir.dt.uint16
U8 = mybir.dt.uint8
FP8X4 = mybir.dt.float8_e4m3fn_x4
ACT = mybir.ActivationFunctionType
MULT = mybir.AluOpType.mult
ADD = mybir.AluOpType.add

P = 128
PACK = 4
K_PASS = P * PACK
PASSES = K // K_PASS
WINDOWS = 2 * PASSES
GROUPS = V // P
HALF = V // 2
LIST_ROWS = 16
BIAS_ROW = D
COLUMNS_KEPT = 8
DIRECT = D - 1

CHUNKS = [[1024, 640, 384], [768, 640, 640], [768, 768, 512], [768, 640, 640]]
SCALAR_COLUMNS = [[0, 0, 0], [384, 128, 0], [0, 256, 0], [0, 128, 128]]
TURN_BANKS, SUM_BANKS = 3, 5
PICKED_BUFS = 4
PRODUCT_BUFS = 24


def tile_picked_bag_lin_gelu_sub_l_kernel(tc, xT, w, b, gate, offs, out):
    nc = tc.nc
    with ExitStack() as ctx:
        keep = ctx.enter_context(tc.tile_pool(name="keep", bufs=1))
        ring = ctx.enter_context(tc.tile_pool(name="ring", bufs=1))
        psum = ctx.enter_context(tc.psum_pool(name="psum", bufs=1))

        offsets = keep.tile([P, D * V // LIST_ROWS], U16, name="offsets")
        ident = keep.tile([P, P], F32, name="ident")
        rows = keep.tile([P, V], F32, name="rows")
        cols = keep.tile([P, GROUPS, COLUMNS_KEPT], F32, name="cols")
        scratch = keep.tile([P, 8], F32, name="scratch")
        windows = [keep.tile([P, T], U32, name="window%d" % q) for q in range(WINDOWS)]
        w_raw = keep.tile([P, PASSES, PACK, N], F32, name="w_raw")
        w_bf = keep.tile([P, PASSES, N, PACK], BF16, name="w_bf", align_bytes=64)
        w_scales = keep.tile([P, PASSES * N], U8, name="w_scales", align_bytes=64)
        x_bf = [keep.tile([P, V, PACK], BF16, name="x_bf%d" % g, align_bytes=64) for g in range(PASSES)]
        x_codes = [keep.tile([P, V], U32, name="x_codes%d" % g, align_bytes=64) for g in range(PASSES)]
        x_scales = [keep.tile([P, V], U8, name="x_scales%d" % g, align_bytes=64) for g in range(PASSES)]
        gate_pairs = keep.tile([P, V, 2], F32, name="gate_pairs")

        nc.gpsimd.memset(rows[:], 0.0)
        raw = {}
        for q in range(WINDOWS):
            g, u = divmod(q, 2)
            pass_rows = xT[g * K_PASS : (g + 1) * K_PASS, :].rearrange("(p t) c -> p t c", t=PACK)
            start = 0
            for c, width in enumerate(CHUNKS[q]):
                chunk = keep.tile([P, 2, width], F32, name="raw%d_%d" % (q, c))
                nc.sync.dma_start(out=chunk[:], in_=pass_rows[:, 2 * u : 2 * u + 2, start : start + width])
                raw[q, c] = (chunk, start)
                start += width
                if (q, c) == (0, 0):
                    nc.sync.dma_start(out=rows[0:D, :], in_=gate[:, 0, :])
                    nc.sync.dma_start(out=rows[BIAS_ROW : BIAS_ROW + 1, 0:N], in_=b.rearrange("n o -> o n"))
                    nc.sync.dma_start(offsets[:], offs)
        for g in range(PASSES):
            nc.sync.dma_start(
                out=w_raw[:, g, :, :], in_=w[g * K_PASS : (g + 1) * K_PASS, :].rearrange("(p t) n -> p t n", t=PACK)
            )

        nc.vector.memset(scratch[:], 0.0)
        nc.scalar.activation(scratch[:, 1:2], scratch[:, 0:1], ACT.Gelu_apprx_tanh)

        make_identity(nc, ident[:])
        turned = psum.tile([P, GROUPS, P], F32, tag="turn", bufs=TURN_BANKS, name="turned")
        for j in range(GROUPS):
            nc.tensor.transpose(turned[:, j, :], rows[:, j * P : (j + 1) * P], ident[:])
        nc.scalar.copy(cols[:], turned[:, :, 0:COLUMNS_KEPT])
        spread = psum.tile([P, V], F32, tag="turn", bufs=TURN_BANKS, name="spread")
        for j in range(GROUPS):
            nc.tensor.transpose(
                spread[:, j * P : (j + 1) * P], cols[:, j, DIRECT : DIRECT + 1].to_broadcast([P, P]), ident[:]
            )
        nc.scalar.copy(gate_pairs[:], spread[:].unsqueeze(2).to_broadcast([P, V, 2]))

        def cast_operands(q, c, first, last):
            chunk, start = raw[q, c]
            pairs = windows[q][:, start + first : start + last].bitcast(BF16).rearrange("p (c i) -> p c i", i=2)
            return pairs, chunk[:, :, first:last].rearrange("p i c -> p c i")

        def cast_w(g):
            nc.gpsimd.tensor_scalar(w_bf[:, g, :, :], w_raw[:, g, :, :].rearrange("p t n -> p n t"), 1.0, 0.0, MULT, ADD)

        def gather(picked, q, entry, count):
            entries = offsets[:, entry // LIST_ROWS : (entry + count) // LIST_ROWS]
            nc.vector.tensor_copy(picked[:], windows[q][:].indirect(entries))

        products = {}

        def weigh(q, d, j, words):
            product = ring.tile([P, 2, P], F32, tag="product", bufs=PRODUCT_BUFS, name="product")
            values = words.bitcast(BF16).rearrange("e (p i) -> e i p", i=2)
            nc.scalar.activation(product[:], values, ACT.Copy, scale=cols[:, j, d : d + 1])
            products[q, d, j] = product

        def turn_and_weigh(q, d, groups, picked):
            bank = psum.tile([P, len(groups), P], F32, tag="turn", bufs=TURN_BANKS, name="turn")
            for s in range(len(groups)):
                nc.tensor.transpose(bank[:, s, :], picked.bitcast(F32)[:, s * P : (s + 1) * P], ident[:])
            for s, j in enumerate(groups):
                weigh(q, d, j, bank[:, s, :])

        def look_up(q, d, groups):
            picked = ring.tile([P, len(groups) * P], U32, tag="picked", bufs=PICKED_BUFS, name="picked")
            gather(picked, q, d * V + groups[0] * P, len(groups) * P)
            turn_and_weigh(q, d, groups, picked[:])

        sums = {}

        def add_up(q, d, groups):
            g, u = divmod(q, 2)
            last_turned = D - 1 if g == 0 else DIRECT - 1
            for j in groups:
                if (u, d) == (0, 0):
                    sums[g, j] = psum.tile([P, PACK, P], F32, tag="sum", bufs=SUM_BANKS, name="sums")
                for i in range(2):
                    nc.tensor.matmul(
                        sums[g, j][:, 2 * u + i, :],
                        products[q, d, j][:, i, :],
                        ident[:],
                        start=((u, d, i) == (0, 0, 0)),
                        stop=((u, d, i) == (1, last_turned, 1)),
                        is_transpose=True,
                    )

        def weigh_direct(direct, u, picked, start, width):
            nc.gpsimd.tensor_tensor(
                direct[:, u, start : start + width, :].rearrange("p v i -> p (v i)"),
                picked[:, start : start + width].bitcast(BF16),
                gate_pairs[:, start : start + width, :].rearrange("p v i -> p (v i)"),
                MULT,
            )

        def round_pass0(j, copy):
            copy(x_bf[0][:, j * P : (j + 1) * P, :], sums[0, j][:].rearrange("p t c -> p c t"))

        def round_pass1(j, direct):
            nc.vector.tensor_tensor(
                x_bf[1][:, j * P : (j + 1) * P, :].rearrange("p c (u i) -> p c u i", i=2),
                sums[1, j][:].rearrange("p (u i) c -> p c u i", i=2),
                direct[:, :, j * P : (j + 1) * P, :].rearrange("p u c i -> p c u i"),
                ADD,
            )

        def quantise_x(g, start, width):
            nc.vector.quantize_mx(
                out=x_codes[g][:, start : start + width].bitcast(FP8X4),
                scales=x_scales[g][:, start : start + width],
                in_=x_bf[g][:, start : start + width, :].rearrange("p v t -> p (v t)"),
            )

        def multiply(acc, w_codes, m, half, g):
            w_cols = slice(g * N + m * P, g * N + (m + 1) * P)
            x_cols = slice(half * HALF, (half + 1) * HALF)
            nc.tensor.matmul_mx(
                out=acc[:],
                lhsT=w_codes[:, w_cols].bitcast(FP8X4),
                lhsT_scale=w_scales[:, w_cols],
                rhs=x_codes[g][:, x_cols].bitcast(FP8X4),
                rhs_scale=x_scales[g][:, x_cols],
                start=(g == 0),
                stop=(g == PASSES - 1),
            )

        def finish(acc, m, half):
            result = keep.tile([P, HALF], F32, name="result%d_%d" % (m, half))
            nc.scalar.activation(result[:], acc[:], ACT.Gelu_apprx_tanh, bias=cols[:, m, BIAS_ROW : BIAS_ROW + 1])
            nc.sync.dma_start(out=out[m * P : (m + 1) * P, half * HALF : (half + 1) * HALF], in_=result[:])

        for c, width in enumerate(CHUNKS[0]):
            nc.vector.tensor_copy(*cast_operands(0, c, 0, width))
        for q in range(1, WINDOWS):
            for c, width in enumerate(CHUNKS[q]):
                split = SCALAR_COLUMNS[q][c]
                nc.gpsimd.tensor_scalar(*cast_operands(q, c, split, width), 1.0, 0.0, MULT, ADD)
                if split > 0:
                    nc.scalar.copy(*cast_operands(q, c, 0, split))

        every, low, high = list(range(GROUPS)), [0, 1], [2, 3]

        pieces = [(q, d) for q in range(2) for d in range(D)]
        for n, (q, d) in enumerate(pieces):
            look_up(q, d, every)
            if n > 0:
                add_up(*pieces[n - 1], every)

        two_pieces = keep.tile([P, 2 * V], U32, name="two_pieces")
        gather(two_pieces, 2, 0, 2 * V)
        turn_and_weigh(2, 0, every, two_pieces[:, 0:V])
        add_up(*pieces[-1], every)
        cast_w(1)
        turn_and_weigh(2, 1, every, two_pieces[:, V : 2 * V])
        held = [keep.tile([P, V], U32, name="held%d" % u) for u in range(2)]
        gather(held[0], 2, DIRECT * V, V)
        direct = keep.tile([P, 2, V, 2], F32, name="direct", tag="raw%d_%d" % (WINDOWS - 1, len(CHUNKS[-1]) - 1))
        weigh_direct(direct, 0, held[0], 0, V)
        round_pass0(0, nc.vector.tensor_copy)
        look_up(2, 2, every)
        round_pass0(1, nc.vector.tensor_copy)
        cast_w(0)

        look_up(3, 0, low)
        round_pass0(2, nc.vector.tensor_copy)
        round_pass0(3, nc.scalar.copy)
        look_up(3, 1, low)
        for d in range(DIRECT):
            add_up(2, d, every)
        add_up(3, 0, low)
        gather(held[1], 3, DIRECT * V, V)
        for half in range(2):
            weigh_direct(direct, 1, held[1], half * HALF, HALF)
        add_up(3, 1, low)
        look_up(3, 2, low)
        look_up(3, 0, high)
        add_up(3, 2, low)
        round_pass1(0, direct)
        look_up(3, 1, high)
        add_up(3, 0, high)
        quantise_x(0, 0, V)

        last = keep.tile([P, HALF], U32, tag="last", name="last", align_bytes=64)
        gather(last, 3, (DIRECT - 1) * V + HALF, HALF)
        for s, j in enumerate(high):
            turn_and_weigh(3, DIRECT - 1, [j], last[:, s * P : (s + 1) * P])
        add_up(3, 1, high)
        w_codes = keep.tile([P, PASSES * N], U32, tag="last", name="w_codes", align_bytes=64)
        nc.vector.quantize_mx(
            out=w_codes[:].bitcast(FP8X4), scales=w_scales[:], in_=w_bf[:].rearrange("p g n t -> p (g n t)")
        )
        round_pass1(1, direct)
        add_up(3, DIRECT - 1, high)

        acc_high = [psum.tile([P, HALF], F32, tag="turn", bufs=TURN_BANKS, name="acc_high") for m in range(N // P)]
        acc_low = [psum.tile([P, HALF], F32, tag="sum", bufs=SUM_BANKS, name="acc_low") for m in range(N // P)]
        quantise_x(1, 0, HALF)
        for m in range(N // P):
            for g in range(PASSES):
                multiply(acc_low[m], w_codes, m, 0, g)
        for m in range(N // P):
            multiply(acc_high[m], w_codes, m, 1, 0)
        for j in high:
            round_pass1(j, direct)
        quantise_x(1, HALF, HALF)
        for m in range(N // P):
            multiply(acc_high[m], w_codes, m, 1, 1)
        for m in range(N // P):
            finish(acc_high[m], m, 1)
        for m in range(N // P):
            finish(acc_low[m], m, 0)
